import numpy as np
import ml_dtypes


def mxq(x, axis, fmt="e4m3"):
    dtype, down = {"e4m3": (ml_dtypes.float8_e4m3fn, 7), "e5m2": (ml_dtypes.float8_e5m2, 14)}[fmt]
    v = np.moveaxis(np.asarray(x, np.float32).astype(ml_dtypes.bfloat16).astype(np.float64), axis, -1)
    blocks = v.reshape(v.shape[:-1] + (-1, 32))
    amax = np.abs(blocks).max(-1, keepdims=True)
    byte = np.maximum(np.where(amax > 0, np.frexp(amax)[1] - 1 + 127, 0) - down, 1)
    scale = np.exp2(byte - 127.0)
    codes = (blocks / scale).astype(np.float32).astype(dtype).astype(np.float64)
    return np.moveaxis((codes * scale).reshape(v.shape), -1, axis)


WIDE = False


def mx_kscale(k):
    if not WIDE:
        return np.ones(k)
    levels = np.array([10, -10, 5, -5, 0])
    if k % 512:
        return np.exp2(np.random.permutation(np.resize(levels, k // 32))).repeat(32)
    a = np.empty((k // 512, 16))
    for p in range(k // 512):
        a[p, :8] = np.random.permutation(np.resize(levels, 8))
        for g in range(8):
            far = levels[np.abs(levels - a[p, g]) >= 10]
            a[p, g + 8] = far[np.random.randint(len(far))]
    return np.exp2(a.ravel()).repeat(32)


def f64(x):
    return np.asarray(x).astype(np.float64)


def striped(idx):
    return np.tile(idx.reshape(-1, 16).T, (8, 1)).astype(np.uint16)


def unstriped(offs):
    return offs[:16].T.reshape(-1).astype(np.int64)


def striped8(idx):
    return np.concatenate([x.reshape(-1, 16).T for x in idx]).astype(np.uint16)


def runs(offs, k):
    lists = np.stack([offs[16 * r : 16 * r + 16].T.reshape(-1) for r in range(8)]).astype(np.int64)
    return lists[np.arange(k) % 512 // 64]


def pack_weight(w):
    k, n = w.shape
    w = f64(np.asarray(w, np.float32).astype(ml_dtypes.bfloat16)).reshape(k // 32, 32, n)
    amax = np.abs(w).max(1)
    byte = np.clip(np.where(amax > 0, np.frexp(amax)[1] - 1 + 127 - 7, 1), 1, 254)
    scaled = (w * np.exp2(127.0 - byte)[:, None, :]).reshape(k, n).astype(np.float32)
    words = np.ascontiguousarray(scaled.reshape(k // 512, 128, 4, n).transpose(0, 1, 3, 2)).astype(ml_dtypes.float8_e4m3fn).view(np.uint8)
    return words, np.ascontiguousarray(byte.astype(np.uint8).reshape(k // 512, 16, n))


def unpack_weight(words, scales):
    g, p, n, _ = words.shape
    vals = np.ascontiguousarray(words).view(ml_dtypes.float8_e4m3fn).astype(np.float64) * np.repeat(np.exp2(scales.astype(np.float64) - 127.0), 8, axis=1)[..., None]
    return vals.transpose(0, 1, 3, 2).reshape(g * 512, n)


def sigmoid(v):
    return 1.0 / (1.0 + np.exp(-np.maximum(v, -700.0)))


K, T, S, G, H, U = 512, 1024, 512, 2048, 512, 1024


def setup_inputs():
    n = np.random.standard_normal
    s = mx_kscale(K)[:, None]
    packed_xT = pack_weight(n((K, T)) * s)
    packed_dT = pack_weight(n((K, G)) / s)
    return {
        "x_words": packed_xT[0],
        "x_scales": packed_xT[1],
        "d_words": packed_dT[0],
        "d_scales": packed_dT[1],
        "gs": (np.random.uniform(0.5, 1.5, (K, 1)) * s).astype(np.float32),
        "mem": n((H, U)).astype(np.float32),
        "offs": striped(np.random.permutation(T)[:S]),
        "k1": striped8(np.random.randint(0, G, (8, H))),
        "n1": striped8(np.stack([np.random.permutation(S) for _ in range(8)])),
        "k2": striped8(np.random.randint(0, G, (8, H))),
        "n2": striped8(np.stack([np.random.permutation(U)[:S] for _ in range(8)])),
    }


def reference(x_words, x_scales, d_words, d_scales, gs, mem, offs, k1, n1, k2, n2):
    d_k2 = unpack_weight(d_words, d_scales)[np.arange(K)[:, None], runs(k2, K)]
    d_k1 = unpack_weight(d_words, d_scales)[np.arange(K)[:, None], runs(k1, K)]
    xq = unpack_weight(x_words, x_scales)[:, unstriped(offs)]
    h = 0.0625 * (d_k1.T @ xq)
    z = f64(gs) * (h * (sigmoid(h[np.arange(H)[:, None], runs(n1, H)])))
    h2 = 0.0625 * ((d_k2.T @ mxq(z, 0, "e4m3")))
    out = f64(mem).copy()
    out[np.arange(H)[:, None], runs(n2, H)] = h2
    return out

@@ -1,0 +1,229 @@
+from contextlib import ExitStack
+
+import concourse.mybir as mybir
+
+K, T, S, G, H, U = 512, 1024, 512, 2048, 512, 1024
+FLOPS = 2 * 2 * K * H * S
+
+F32 = mybir.dt.float32
+BF16 = mybir.dt.bfloat16
+I32 = mybir.dt.int32
+U32 = mybir.dt.uint32
+U16 = mybir.dt.uint16
+U8 = mybir.dt.uint8
+FP8X4 = mybir.dt.float8_e4m3fn_x4
+MULT = mybir.AluOpType.mult
+COPY = mybir.ActivationFunctionType.Copy
+SIGMOID = mybir.ActivationFunctionType.Sigmoid
+
+P = 128
+PACK = 4
+SIXTEENTH = 0.0625
+PAGE_BYTES = 4 * U
+CHUNKS = ((0, 128), (128, 128), (256, 256))
+
+
+def tile_picked_codegatepage_none_p_kernel(
+    tc, x_words, x_scales, d_words, d_scales, gs, mem, offs, k1, n1, k2, n2, out
+):
+    nc = tc.nc
+    with ExitStack() as ctx:
+        lists = ctx.enter_context(tc.tile_pool(name="lists", bufs=1))
+        keep = ctx.enter_context(tc.tile_pool(name="keep", bufs=1))
+        shared = ctx.enter_context(tc.tile_pool(name="shared", bufs=1))
+        psum = ctx.enter_context(tc.psum_pool(name="psum", bufs=1))
+
+        def tile(shape, dtype, name, tag=None):
+            return keep.tile(shape, dtype, name=name, tag=tag or name, align_bytes=64)
+
+        def tile_at(offset, shape, dtype, name):
+            return shared.tile(shape, dtype, name=name, offset=offset, align_bytes=64)
+
+        def load_scale_rows(name, src, width):
+            rows = tile([P, width], U8, name)
+            words = src[0].bitcast(I32).unsqueeze(1).to_broadcast([16, 8, width // 4])
+            nc.sync.dma_start(rows[:].bitcast(I32), words)
+            return rows
+
+        def load_list(src, name):
+            held = lists.tile([P, S // 16], U16, name=name)
+            nc.sync.dma_start(held[:], src)
+            return held
+
+        def zeroed_bytes(width, name):
+            plane = tile([P, width], U8, name)
+            nc.vector.memset(plane[:].bitcast(I32), 0)
+            return plane
+
+        def move_rows(queue, placed, picked):
+            for q in range(4):
+                queue.dma_start(
+                    placed[:].bitcast(I32)[32 * q : 32 * q + 4, :],
+                    picked[:].bitcast(I32)[32 * q : 32 * q + 32 : 8, :],
+                )
+
+        def deal(dst, src):
+            nc.vector.tensor_copy(
+                dst.rearrange("p (t m) -> p m t", t=PACK), src.rearrange("p (m t) -> p m t", t=PACK)
+            )
+
+        warm_in = tile([P, 1], F32, "warm_in")
+        nc.vector.memset(warm_in[:], 0.0)
+        warm = tile([P, 1], F32, "warm")
+        nc.scalar.activation(warm[:], warm_in[:], SIGMOID)
+        placed1 = zeroed_bytes(H, "placed1")
+        placed2 = zeroed_bytes(H, "placed2")
+
+        k1_list = load_list(k1, "k1_list")
+        d_bytes = load_scale_rows("d_bytes", d_scales, G)
+        offs_list = load_list(offs, "offs_list")
+        x_bytes = tile([P, T], U8, "x_bytes")
+        for q in range(4):
+            rows = x_scales[0].bitcast(I32)[4 * q : 4 * q + 4, :]
+            nc.sync.dma_start(
+                x_bytes[:].bitcast(I32)[32 * q : 32 * q + 32, :], rows.unsqueeze(0).to_broadcast([8, 4, T // 4])
+            )
+        x_table = tile([P, T], I32, "x_table")
+        nc.sync.dma_start(x_table[:], x_words[0].rearrange("p n t -> p (n t)").bitcast(I32))
+        d_table = tile([P, G], I32, "d_table")
+        nc.sync.dma_start(d_table[:], d_words[0].rearrange("p n t -> p (n t)").bitcast(I32))
+        k2_list = load_list(k2, "k2_list")
+        n1_list = load_list(n1, "n1_list")
+        n2_list = load_list(n2, "n2_list")
+
+        w1_bytes = tile([P, H], U8, "w1_bytes")
+        nc.vector.tensor_copy(w1_bytes[:], d_bytes[:].indirect(k1_list[:]))
+        staged1 = tile_at(PAGE_BYTES - 256, [P, H], U8, "staged1")
+        deal(staged1[:], w1_bytes[:])
+        move_rows(nc.scalar, placed1, staged1)
+        xq_bytes = tile([P, S], U8, "xq_bytes")
+        nc.vector.tensor_copy(xq_bytes[:], x_bytes[:].indirect(offs_list[:]))
+        gain = tile([P, PACK], F32, "gain")
+        nc.scalar.dma_start(gain[:], gs.rearrange("(p t) o -> p (t o)", t=PACK))
+
+        x_codes = tile([P, S], U32, "x_codes")
+        nc.vector.tensor_copy(x_codes[:], x_table[:].bitcast(U32).indirect(offs_list[:]))
+        w1_picked = tile_at(4 * PAGE_BYTES, [P, H], U32, "w1_picked")
+        nc.vector.tensor_copy(w1_picked[:], d_table[:].bitcast(U32).indirect(k1_list[:]))
+        w1_codes = tile([P, H], U32, "w1_codes")
+        deal(w1_codes[:], w1_picked[:])
+
+        mem_rows = mem.rearrange("(p t) u -> t p u", t=PACK)
+        out_rows = out.rearrange("(p t) u -> t p u", t=PACK)
+        pages = []
+
+        def load_page(t):
+            page = tile_at(t * PAGE_BYTES, [P, U], F32, "page%d" % t)
+            nc.sync.dma_start(page[:], mem_rows[t])
+            pages.append(page)
+
+        load_page(0)
+        load_page(1)
+
+        h_rows = []
+        for t in range(PACK):
+            cols = slice(P * t, P * (t + 1))
+            acc = psum.tile([P, S], F32, name="h_bank%d" % t)
+            nc.tensor.matmul_mx(
+                acc[:], lhsT=w1_codes[:, cols].bitcast(FP8X4), lhsT_scale=placed1[:, cols],
+                rhs=x_codes[:].bitcast(FP8X4), rhs_scale=xq_bytes[:], start=True, stop=True,
+            )
+            h_t = tile([P, S], F32, "h_row%d" % t)
+            nc.scalar.activation(h_t[:], acc[:], COPY, scale=SIXTEENTH)
+            h_rows.append(h_t)
+
+        w2_bytes = tile_at(4 * PAGE_BYTES, [P, H], U8, "w2_bytes")
+        nc.vector.tensor_copy(w2_bytes[:], d_bytes[:].indirect(k2_list[:]))
+        staged2 = tile_at(3 * PAGE_BYTES - 256, [P, H], U8, "staged2")
+        deal(staged2[:], w2_bytes[:])
+        move_rows(nc.sync, placed2, staged2)
+        w2_picked = tile_at(4 * PAGE_BYTES + 512, [P, H], U32, "w2_picked")
+        nc.vector.tensor_copy(w2_picked[:], d_table[:].bitcast(U32).indirect(k2_list[:]))
+        w2_codes = tile([P, H], U32, "w2_codes")
+        deal(w2_codes[:], w2_picked[:])
+        load_page(2)
+        load_page(3)
+
+        weighted = tile([P, PACK, S], F32, "weighted")
+        for t in range(PACK):
+            nc.vector.tensor_scalar(weighted[:, t, :], h_rows[t][:], gain[:, t : t + 1], None, MULT)
+
+        def gate(c, gates):
+            j0, n = CHUNKS[c]
+            for t in range(PACK):
+                nc.scalar.activation(
+                    gates[:, t, :], h_rows[t][:].indirect(n1_list[:, j0 // 16 : (j0 + n) // 16]), SIGMOID
+                )
+
+        def quantise(c, gates, z, z_codes):
+            j0, n = CHUNKS[c]
+            nc.vector.tensor_tensor(
+                z[:].rearrange("p (c i) t -> p c t i", i=4),
+                weighted[:, :, j0 : j0 + n].rearrange("p t (c i) -> p c t i", i=4),
+                gates[:].rearrange("p t (c i) -> p c t i", i=4),
+                MULT,
+            )
+            z_scales = tile([P, n], U8, "z_scales%d" % c)
+            nc.vector.quantize_mx(z_codes[:].bitcast(FP8X4), z_scales[:], z[:].rearrange("p n t -> p (n t)"))
+            return z_scales
+
+        def product(acc, t, z_codes, z_scales):
+            cols = slice(P * t, P * (t + 1))
+            nc.tensor.matmul_mx(
+                acc, lhsT=w2_codes[:, cols].bitcast(FP8X4), lhsT_scale=placed2[:, cols],
+                rhs=z_codes[:].bitcast(FP8X4), rhs_scale=z_scales[:], start=True, stop=True,
+            )
+
+        def scatter(c, t, values):
+            j0, n = CHUNKS[c]
+            nc.vector.tensor_copy(pages[t][:].indirect(n2_list[:, j0 // 16 : (j0 + n) // 16]), values)
+
+        base = 4 * PAGE_BYTES + 4096
+        gates0 = tile([P, PACK, 128], F32, "gates0")
+        gate(0, gates0)
+        gates1 = tile([P, PACK, 128], F32, "gates1")
+        gate(1, gates1)
+        z0 = tile([P, 128, PACK], BF16, "z0")
+        codes0 = tile_at(base, [P, 128], U32, "codes0")
+        scales0 = quantise(0, gates0, z0, codes0)
+        acc0, h2_0 = [], []
+        for t in range(PACK):
+            acc = psum.tile([P, 128], F32, name="h2_bank0_%d" % t, tag="h_bank%d" % t)
+            product(acc[:], t, codes0, scales0)
+            acc0.append(acc)
+        for t in range(PACK - 1):
+            if t == 2:
+                values = tile_at(base + 4096, [P, 128], F32, "h2_0_2")
+            else:
+                values = tile([P, 128], F32, "h2_0_%d" % t)
+            nc.scalar.activation(values[:], acc0[t][:], COPY, scale=SIXTEENTH)
+            h2_0.append(values)
+        z1 = tile([P, 128, PACK], BF16, "z1")
+        codes1 = tile([P, 128], U32, "codes1")
+        scales1 = quantise(1, gates1, z1, codes1)
+        acc1 = psum.tile([P, PACK, 128], F32, name="h2_bank1")
+        for t in range(PACK):
+            product(acc1[:, t, :], t, codes1, scales1)
+        gates2 = tile_at(base, [P, PACK, 256], F32, "gates2")
+        gate(2, gates2)
+        for t in range(PACK - 1):
+            scatter(0, t, h2_0[t][:])
+        z2 = tile_at(base + 4096, [P, 256, PACK], BF16, "z2")
+        codes2 = tile([P, 256], U32, "codes2")
+        scales2 = quantise(2, gates2, z2, codes2)
+        last0 = tile_at(base, [P, 128], F32, "h2_0_3")
+        nc.scalar.activation(last0[:], acc0[3][:], COPY, scale=SIXTEENTH)
+        h2_1 = tile_at(base + 4096, [P, PACK, 128], F32, "h2_1")
+        nc.scalar.activation(h2_1[:], acc1[:], COPY, scale=SIXTEENTH)
+        h2_2 = tile([P, PACK, 256], F32, "h2_2")
+        for b in range(2):
+            acc = psum.tile([P, 2, 256], F32, name="h2_bank2_%d" % b)
+            for i in range(2):
+                product(acc[:, i, :], 2 * b + i, codes2, scales2)
+            nc.scalar.activation(h2_2[:, 2 * b : 2 * b + 2, :], acc[:], COPY, scale=SIXTEENTH)
+        scatter(0, 3, last0[:])
+        for t in range(PACK):
+            scatter(1, t, h2_1[:, t, :])
+        for t in range(PACK):
+            scatter(2, t, h2_2[:, t, :])
+            nc.sync.dma_start(out_rows[t], pages[t][:])

@@ -18,9 +18,9 @@ SIGMOID = mybir.ActivationFunctionType.Sigmoid
 
 P = 128
 PACK = 4
+RUN = 8
 SIXTEENTH = 0.0625
 PAGE_BYTES = 4 * U
-CHUNKS = ((0, 128), (128, 128), (256, 256))
 
 
 def tile_picked_codegatepage_none_p_kernel(
@@ -67,10 +67,11 @@ def tile_picked_codegatepage_none_p_kernel(
                 dst.rearrange("p (t m) -> p m t", t=PACK), src.rearrange("p (m t) -> p m t", t=PACK)
             )
 
-        warm_in = tile([P, 1], F32, "warm_in")
-        nc.vector.memset(warm_in[:], 0.0)
-        warm = tile([P, 1], F32, "warm")
-        nc.scalar.activation(warm[:], warm_in[:], SIGMOID)
+        def deal_runs(dst, src, run):
+            nc.vector.tensor_copy(
+                dst.rearrange("p (t a b) -> p a t b", t=PACK, b=run), src.rearrange("p (a t b) -> p a t b", t=PACK, b=run)
+            )
+
         placed1 = zeroed_bytes(H, "placed1")
         placed2 = zeroed_bytes(H, "placed2")
 
@@ -83,33 +84,37 @@ def tile_picked_codegatepage_none_p_kernel(
             nc.sync.dma_start(
                 x_bytes[:].bitcast(I32)[32 * q : 32 * q + 32, :], rows.unsqueeze(0).to_broadcast([8, 4, T // 4])
             )
-        x_table = tile([P, T], I32, "x_table")
-        nc.sync.dma_start(x_table[:], x_words[0].rearrange("p n t -> p (n t)").bitcast(I32))
         d_table = tile([P, G], I32, "d_table")
         nc.sync.dma_start(d_table[:], d_words[0].rearrange("p n t -> p (n t)").bitcast(I32))
+        x_table = tile_at(4 * PAGE_BYTES, [P, T], I32, "x_table")
+        nc.sync.dma_start(x_table[:], x_words[0].rearrange("p n t -> p (n t)").bitcast(I32))
         k2_list = load_list(k2, "k2_list")
         n1_list = load_list(n1, "n1_list")
         n2_list = load_list(n2, "n2_list")
 
-        w1_bytes = tile([P, H], U8, "w1_bytes")
+        warm_in = tile([P, 1], F32, "warm_in")
+        nc.vector.memset(warm_in[:], 0.0)
+        warm = tile([P, 1], F32, "warm")
+        nc.scalar.activation(warm[:], warm_in[:], SIGMOID)
+
+        w1_bytes = tile_at(5 * PAGE_BYTES, [P, H], U8, "w1_bytes")
         nc.vector.tensor_copy(w1_bytes[:], d_bytes[:].indirect(k1_list[:]))
         staged1 = tile_at(PAGE_BYTES - 256, [P, H], U8, "staged1")
         deal(staged1[:], w1_bytes[:])
         move_rows(nc.scalar, placed1, staged1)
+        gain = tile_at(5 * PAGE_BYTES, [P, PACK], F32, "gain")
+        nc.scalar.dma_start(gain[:], gs.rearrange("(p t) o -> p (t o)", t=PACK))
         xq_bytes = tile([P, S], U8, "xq_bytes")
         nc.vector.tensor_copy(xq_bytes[:], x_bytes[:].indirect(offs_list[:]))
-        gain = tile([P, PACK], F32, "gain")
-        nc.scalar.dma_start(gain[:], gs.rearrange("(p t) o -> p (t o)", t=PACK))
-
-        x_codes = tile([P, S], U32, "x_codes")
-        nc.vector.tensor_copy(x_codes[:], x_table[:].bitcast(U32).indirect(offs_list[:]))
-        w1_picked = tile_at(4 * PAGE_BYTES, [P, H], U32, "w1_picked")
+        w1_picked = tile([P, H], U32, "w1_picked")
         nc.vector.tensor_copy(w1_picked[:], d_table[:].bitcast(U32).indirect(k1_list[:]))
         w1_codes = tile([P, H], U32, "w1_codes")
         deal(w1_codes[:], w1_picked[:])
+        x_codes = tile([P, S], U32, "x_codes")
+        nc.vector.tensor_copy(x_codes[:], x_table[:].bitcast(U32).indirect(offs_list[:]))
 
-        mem_rows = mem.rearrange("(p t) u -> t p u", t=PACK)
-        out_rows = out.rearrange("(p t) u -> t p u", t=PACK)
+        mem_rows = mem.rearrange("(a t b) u -> t a b u", t=PACK, b=RUN)
+        out_rows = out.rearrange("(a t b) u -> t a b u", t=PACK, b=RUN)
         pages = []
 
         def load_page(t):
@@ -129,37 +134,41 @@ def tile_picked_codegatepage_none_p_kernel(
                 rhs=x_codes[:].bitcast(FP8X4), rhs_scale=xq_bytes[:], start=True, stop=True,
             )
             h_t = tile([P, S], F32, "h_row%d" % t)
-            nc.scalar.activation(h_t[:], acc[:], COPY, scale=SIXTEENTH)
+            if t == 1:
+                nc.vector.tensor_scalar(h_t[:], acc[:], SIXTEENTH, None, MULT)
+            else:
+                nc.scalar.activation(h_t[:], acc[:], COPY, scale=SIXTEENTH)
             h_rows.append(h_t)
 
         w2_bytes = tile_at(4 * PAGE_BYTES, [P, H], U8, "w2_bytes")
         nc.vector.tensor_copy(w2_bytes[:], d_bytes[:].indirect(k2_list[:]))
         staged2 = tile_at(3 * PAGE_BYTES - 256, [P, H], U8, "staged2")
-        deal(staged2[:], w2_bytes[:])
+        deal_runs(staged2[:].bitcast(I32), w2_bytes[:].bitcast(I32), RUN // 4)
         move_rows(nc.sync, placed2, staged2)
         w2_picked = tile_at(4 * PAGE_BYTES + 512, [P, H], U32, "w2_picked")
         nc.vector.tensor_copy(w2_picked[:], d_table[:].bitcast(U32).indirect(k2_list[:]))
         w2_codes = tile([P, H], U32, "w2_codes")
-        deal(w2_codes[:], w2_picked[:])
+        deal_runs(w2_codes[:], w2_picked[:], RUN)
         load_page(2)
         load_page(3)
 
-        weighted = tile([P, PACK, S], F32, "weighted")
-        for t in range(PACK):
-            nc.vector.tensor_scalar(weighted[:, t, :], h_rows[t][:], gain[:, t : t + 1], None, MULT)
+        def weigh(engine, j0, n, weighted):
+            for t in range(PACK):
+                if engine is nc.vector:
+                    nc.vector.tensor_scalar(weighted[:, t, :], h_rows[t][:, j0 : j0 + n], gain[:, t : t + 1], None, MULT)
+                else:
+                    nc.scalar.activation(weighted[:, t, :], h_rows[t][:, j0 : j0 + n], COPY, scale=gain[:, t : t + 1])
 
-        def gate(c, gates):
-            j0, n = CHUNKS[c]
+        def gate(j0, n, gates):
             for t in range(PACK):
                 nc.scalar.activation(
                     gates[:, t, :], h_rows[t][:].indirect(n1_list[:, j0 // 16 : (j0 + n) // 16]), SIGMOID
                 )
 
-        def quantise(c, gates, z, z_codes):
-            j0, n = CHUNKS[c]
+        def quantise(c, n, weighted, gates, z, z_codes):
             nc.vector.tensor_tensor(
                 z[:].rearrange("p (c i) t -> p c t i", i=4),
-                weighted[:, :, j0 : j0 + n].rearrange("p t (c i) -> p c t i", i=4),
+                weighted[:].rearrange("p t (c i) -> p c t i", i=4),
                 gates[:].rearrange("p t (c i) -> p c t i", i=4),
                 MULT,
             )
@@ -174,56 +183,57 @@ def tile_picked_codegatepage_none_p_kernel(
                 rhs=z_codes[:].bitcast(FP8X4), rhs_scale=z_scales[:], start=True, stop=True,
             )
 
-        def scatter(c, t, values):
-            j0, n = CHUNKS[c]
+        def scatter(j0, n, t, values):
             nc.vector.tensor_copy(pages[t][:].indirect(n2_list[:, j0 // 16 : (j0 + n) // 16]), values)
 
-        base = 4 * PAGE_BYTES + 4096
-        gates0 = tile([P, PACK, 128], F32, "gates0")
-        gate(0, gates0)
-        gates1 = tile([P, PACK, 128], F32, "gates1")
-        gate(1, gates1)
+        base = 6 * PAGE_BYTES
+        weighted0 = tile([P, PACK, 128], F32, "weighted0")
+        weigh(nc.vector, 0, 128, weighted0)
+        gates0 = tile_at(base, [P, PACK, 128], F32, "gates0")
+        gate(0, 128, gates0)
+        gates1 = tile_at(4 * PAGE_BYTES + 512, [P, PACK, 128], F32, "gates1")
+        gate(128, 128, gates1)
         z0 = tile([P, 128, PACK], BF16, "z0")
-        codes0 = tile_at(base, [P, 128], U32, "codes0")
-        scales0 = quantise(0, gates0, z0, codes0)
-        acc0, h2_0 = [], []
+        codes0 = tile_at(base + PAGE_BYTES, [P, 128], U32, "codes0")
+        scales0 = quantise(0, 128, weighted0, gates0, z0, codes0)
+        h2_0 = []
         for t in range(PACK):
             acc = psum.tile([P, 128], F32, name="h2_bank0_%d" % t, tag="h_bank%d" % t)
             product(acc[:], t, codes0, scales0)
-            acc0.append(acc)
-        for t in range(PACK - 1):
-            if t == 2:
-                values = tile_at(base + 4096, [P, 128], F32, "h2_0_2")
-            else:
-                values = tile([P, 128], F32, "h2_0_%d" % t)
-            nc.scalar.activation(values[:], acc0[t][:], COPY, scale=SIXTEENTH)
+            values = tile([P, 128], F32, "h2_0_%d" % t)
+            nc.scalar.activation(values[:], acc[:], COPY, scale=SIXTEENTH)
             h2_0.append(values)
+        weighted1 = tile_at(base, [P, PACK, 128], F32, "weighted1")
+        weigh(nc.vector, 128, 128, weighted1)
         z1 = tile([P, 128, PACK], BF16, "z1")
-        codes1 = tile([P, 128], U32, "codes1")
-        scales1 = quantise(1, gates1, z1, codes1)
-        acc1 = psum.tile([P, PACK, 128], F32, name="h2_bank1")
+        codes1 = tile_at(base + 2 * PAGE_BYTES, [P, 128], U32, "codes1")
+        scales1 = quantise(1, 128, weighted1, gates1, z1, codes1)
+        acc1 = [psum.tile([P, 2, 128], F32, name="h2_bank1_%d" % b) for b in range(2)]
         for t in range(PACK):
-            product(acc1[:, t, :], t, codes1, scales1)
-        gates2 = tile_at(base, [P, PACK, 256], F32, "gates2")
-        gate(2, gates2)
-        for t in range(PACK - 1):
-            scatter(0, t, h2_0[t][:])
-        z2 = tile_at(base + 4096, [P, 256, PACK], BF16, "z2")
+            product(acc1[t // 2][:, t % 2, :], t, codes1, scales1)
+        weighted2 = tile_at(base + PAGE_BYTES, [P, PACK, 256], F32, "weighted2")
+        weigh(nc.scalar, 256, 256, weighted2)
+        h2_1a = tile_at(base + 3 * PAGE_BYTES, [P, 2, 128], F32, "h2_1a")
+        nc.scalar.activation(h2_1a[:], acc1[0][:], COPY, scale=SIXTEENTH)
+        gates2 = tile_at(base + 2 * PAGE_BYTES, [P, PACK, 256], F32, "gates2")
+        gate(256, 256, gates2)
+        for t in range(PACK):
+            scatter(0, 128, t, h2_0[t][:])
+        for t in range(2):
+            scatter(128, 128, t, h2_1a[:, t, :])
+        z2 = tile_at(base + 3 * PAGE_BYTES, [P, 256, PACK], BF16, "z2")
         codes2 = tile([P, 256], U32, "codes2")
-        scales2 = quantise(2, gates2, z2, codes2)
-        last0 = tile_at(base, [P, 128], F32, "h2_0_3")
-        nc.scalar.activation(last0[:], acc0[3][:], COPY, scale=SIXTEENTH)
-        h2_1 = tile_at(base + 4096, [P, PACK, 128], F32, "h2_1")
-        nc.scalar.activation(h2_1[:], acc1[:], COPY, scale=SIXTEENTH)
+        scales2 = quantise(2, 256, weighted2, gates2, z2, codes2)
+        h2_1b = tile_at(base + 2 * PAGE_BYTES, [P, 2, 128], F32, "h2_1b")
+        nc.scalar.activation(h2_1b[:], acc1[1][:], COPY, scale=SIXTEENTH)
         h2_2 = tile([P, PACK, 256], F32, "h2_2")
         for b in range(2):
             acc = psum.tile([P, 2, 256], F32, name="h2_bank2_%d" % b)
             for i in range(2):
                 product(acc[:, i, :], 2 * b + i, codes2, scales2)
             nc.scalar.activation(h2_2[:, 2 * b : 2 * b + 2, :], acc[:], COPY, scale=SIXTEENTH)
-        scatter(0, 3, last0[:])
+        for t in range(2, PACK):
+            scatter(128, 128, t, h2_1b[:, t - 2, :])
         for t in range(PACK):
-            scatter(1, t, h2_1[:, t, :])
-        for t in range(PACK):
-            scatter(2, t, h2_2[:, t, :])
+            scatter(256, 256, t, h2_2[:, t, :])
             nc.sync.dma_start(out_rows[t], pages[t][:])

@@ -13,6 +13,7 @@ U16 = mybir.dt.uint16
 U8 = mybir.dt.uint8
 FP8X4 = mybir.dt.float8_e4m3fn_x4
 MULT = mybir.AluOpType.mult
+ADD = mybir.AluOpType.add
 COPY = mybir.ActivationFunctionType.Copy
 SIGMOID = mybir.ActivationFunctionType.Sigmoid
 
@@ -42,7 +43,7 @@ def tile_picked_codegatepage_none_p_kernel(
         def load_scale_rows(name, src, width):
             rows = tile([P, width], U8, name)
             words = src[0].bitcast(I32).unsqueeze(1).to_broadcast([16, 8, width // 4])
-            nc.sync.dma_start(rows[:].bitcast(I32), words)
+            nc.scalar.dma_start(rows[:].bitcast(I32), words)
             return rows
 
         def load_list(src, name):
@@ -157,7 +158,7 @@ def tile_picked_codegatepage_none_p_kernel(
                 if engine is nc.vector:
                     nc.vector.tensor_scalar(weighted[:, t, :], h_rows[t][:, j0 : j0 + n], gain[:, t : t + 1], None, MULT)
                 else:
-                    nc.scalar.activation(weighted[:, t, :], h_rows[t][:, j0 : j0 + n], COPY, scale=gain[:, t : t + 1])
+                    nc.gpsimd.tensor_scalar(weighted[:, t, :], h_rows[t][:, j0 : j0 + n], gain[:, t : t + 1], 0.0, MULT, ADD)
 
         def gate(j0, n, gates):
             for t in range(PACK):
@@ -165,13 +166,15 @@ def tile_picked_codegatepage_none_p_kernel(
                     gates[:, t, :], h_rows[t][:].indirect(n1_list[:, j0 // 16 : (j0 + n) // 16]), SIGMOID
                 )
 
-        def quantise(c, n, weighted, gates, z, z_codes):
-            nc.vector.tensor_tensor(
-                z[:].rearrange("p (c i) t -> p c t i", i=4),
-                weighted[:].rearrange("p t (c i) -> p c t i", i=4),
-                gates[:].rearrange("p t (c i) -> p c t i", i=4),
+        def gated(engine, weighted, gates, z):
+            engine.tensor_tensor(
+                z.rearrange("p (c i) t -> p c t i", i=4),
+                weighted.rearrange("p t (c i) -> p c t i", i=4),
+                gates.rearrange("p t (c i) -> p c t i", i=4),
                 MULT,
             )
+
+        def quantise(c, n, z, z_codes):
             z_scales = tile([P, n], U8, "z_scales%d" % c)
             nc.vector.quantize_mx(z_codes[:].bitcast(FP8X4), z_scales[:], z[:].rearrange("p n t -> p (n t)"))
             return z_scales
@@ -195,7 +198,8 @@ def tile_picked_codegatepage_none_p_kernel(
         gate(128, 128, gates1)
         z0 = tile([P, 128, PACK], BF16, "z0")
         codes0 = tile_at(base + PAGE_BYTES, [P, 128], U32, "codes0")
-        scales0 = quantise(0, 128, weighted0, gates0, z0, codes0)
+        gated(nc.vector, weighted0[:], gates0[:], z0[:])
+        scales0 = quantise(0, 128, z0, codes0)
         h2_0 = []
         for t in range(PACK):
             acc = psum.tile([P, 128], F32, name="h2_bank0_%d" % t, tag="h_bank%d" % t)
@@ -205,35 +209,42 @@ def tile_picked_codegatepage_none_p_kernel(
             h2_0.append(values)
         weighted1 = tile_at(base, [P, PACK, 128], F32, "weighted1")
         weigh(nc.vector, 128, 128, weighted1)
-        z1 = tile([P, 128, PACK], BF16, "z1")
-        codes1 = tile_at(base + 2 * PAGE_BYTES, [P, 128], U32, "codes1")
-        scales1 = quantise(1, 128, weighted1, gates1, z1, codes1)
-        acc1 = [psum.tile([P, 2, 128], F32, name="h2_bank1_%d" % b) for b in range(2)]
-        for t in range(PACK):
-            product(acc1[t // 2][:, t % 2, :], t, codes1, scales1)
+        z1 = tile_at(base + PAGE_BYTES + 1024, [P, 128, PACK], BF16, "z1")
+        codes1 = tile_at(base + 2 * PAGE_BYTES + 2048 - 256, [P, 128], U32, "codes1")
+        gated(nc.vector, weighted1[:], gates1[:], z1[:])
+        scales1 = quantise(1, 128, z1, codes1)
+        acc1a = psum.tile([P, 3, 128], F32, name="h2_bank1a")
+        acc1b = psum.tile([P, 128], F32, name="h2_bank1b")
+        for t in range(PACK - 1):
+            product(acc1a[:, t, :], t, codes1, scales1)
+        product(acc1b[:], PACK - 1, codes1, scales1)
         weighted2 = tile_at(base + PAGE_BYTES, [P, PACK, 256], F32, "weighted2")
-        weigh(nc.scalar, 256, 256, weighted2)
-        h2_1a = tile_at(base + 3 * PAGE_BYTES, [P, 2, 128], F32, "h2_1a")
-        nc.scalar.activation(h2_1a[:], acc1[0][:], COPY, scale=SIXTEENTH)
-        gates2 = tile_at(base + 2 * PAGE_BYTES, [P, PACK, 256], F32, "gates2")
-        gate(256, 256, gates2)
+        weigh(nc.gpsimd, 256, 256, weighted2)
+        h2_1a = tile_at(base + 3 * PAGE_BYTES, [P, 3, 128], F32, "h2_1a")
+        nc.scalar.activation(h2_1a[:], acc1a[:], COPY, scale=SIXTEENTH)
+        gates2 = tile_at(base + 2 * PAGE_BYTES, [P, PACK, 128], F32, "gates2")
+        gate(256, 128, gates2)
+        gates3 = tile_at(base + 2 * PAGE_BYTES + 2048, [P, PACK, 128], F32, "gates3")
+        gate(384, 128, gates3)
         for t in range(PACK):
             scatter(0, 128, t, h2_0[t][:])
-        for t in range(2):
+        z2 = tile([P, 256, PACK], BF16, "z2")
+        gated(nc.gpsimd, weighted2[:, :, :128], gates2[:], z2[:, :128, :])
+        gated(nc.gpsimd, weighted2[:, :, 128:], gates3[:], z2[:, 128:, :])
+        for t in range(PACK - 1):
             scatter(128, 128, t, h2_1a[:, t, :])
-        z2 = tile_at(base + 3 * PAGE_BYTES, [P, 256, PACK], BF16, "z2")
-        codes2 = tile([P, 256], U32, "codes2")
-        scales2 = quantise(2, 256, weighted2, gates2, z2, codes2)
-        h2_1b = tile_at(base + 2 * PAGE_BYTES, [P, 2, 128], F32, "h2_1b")
-        nc.scalar.activation(h2_1b[:], acc1[1][:], COPY, scale=SIXTEENTH)
-        h2_2 = tile([P, PACK, 256], F32, "h2_2")
-        for b in range(2):
-            acc = psum.tile([P, 2, 256], F32, name="h2_bank2_%d" % b)
-            for i in range(2):
-                product(acc[:, i, :], 2 * b + i, codes2, scales2)
-            nc.scalar.activation(h2_2[:, 2 * b : 2 * b + 2, :], acc[:], COPY, scale=SIXTEENTH)
-        for t in range(2, PACK):
-            scatter(128, 128, t, h2_1b[:, t - 2, :])
+        codes2 = tile_at(base + 3 * PAGE_BYTES, [P, 256], U32, "codes2")
+        scales2 = quantise(2, 256, z2, codes2)
+        h2_1b = tile_at(base + 2 * PAGE_BYTES + 2048, [P, 128], F32, "h2_1b")
+        nc.scalar.activation(h2_1b[:], acc1b[:], COPY, scale=SIXTEENTH)
+        h2_2 = []
         for t in range(PACK):
-            scatter(256, 256, t, h2_2[:, t, :])
+            acc = psum.tile([P, 256], F32, name="h2_bank2_%d" % t, tag="h_bank%d" % t)
+            product(acc[:], t, codes2, scales2)
+            values = tile([P, 256], F32, "h2_2_%d" % t)
+            nc.scalar.activation(values[:], acc[:], COPY, scale=SIXTEENTH)
+            h2_2.append(values)
+        scatter(128, 128, PACK - 1, h2_1b[:])
+        for t in range(PACK):
+            scatter(256, 256, t, h2_2[t][:])
             nc.sync.dma_start(out_rows[t], pages[t][:])

from contextlib import ExitStack

import concourse.mybir as mybir

K, T, S, G, H, U = 512, 1024, 512, 2048, 512, 1024
FLOPS = 2 * 2 * K * H * S

F32 = mybir.dt.float32
BF16 = mybir.dt.bfloat16
I32 = mybir.dt.int32
U32 = mybir.dt.uint32
U16 = mybir.dt.uint16
U8 = mybir.dt.uint8
FP8X4 = mybir.dt.float8_e4m3fn_x4
MULT = mybir.AluOpType.mult
ADD = mybir.AluOpType.add
COPY = mybir.ActivationFunctionType.Copy
SIGMOID = mybir.ActivationFunctionType.Sigmoid

P = 128
PACK = 4
RUN = 8
SIXTEENTH = 0.0625
PAGE_BYTES = 4 * U


def tile_picked_codegatepage_none_p_kernel(
    tc, x_words, x_scales, d_words, d_scales, gs, mem, offs, k1, n1, k2, n2, out
):
    nc = tc.nc
    with ExitStack() as ctx:
        lists = ctx.enter_context(tc.tile_pool(name="lists", bufs=1))
        keep = ctx.enter_context(tc.tile_pool(name="keep", bufs=1))
        shared = ctx.enter_context(tc.tile_pool(name="shared", bufs=1))
        psum = ctx.enter_context(tc.psum_pool(name="psum", bufs=1))

        def tile(shape, dtype, name, tag=None):
            return keep.tile(shape, dtype, name=name, tag=tag or name, align_bytes=64)

        def tile_at(offset, shape, dtype, name):
            return shared.tile(shape, dtype, name=name, offset=offset, align_bytes=64)

        def load_scale_rows(name, src, width):
            rows = tile([P, width], U8, name)
            words = src[0].bitcast(I32).unsqueeze(1).to_broadcast([16, 8, width // 4])
            nc.scalar.dma_start(rows[:].bitcast(I32), words)
            return rows

        def load_list(src, name):
            held = lists.tile([P, S // 16], U16, name=name)
            nc.sync.dma_start(held[:], src)
            return held

        def zeroed_bytes(width, name):
            plane = tile([P, width], U8, name)
            nc.vector.memset(plane[:].bitcast(I32), 0)
            return plane

        def move_rows(queue, placed, picked):
            for q in range(4):
                queue.dma_start(
                    placed[:].bitcast(I32)[32 * q : 32 * q + 4, :],
                    picked[:].bitcast(I32)[32 * q : 32 * q + 32 : 8, :],
                )

        def deal(dst, src):
            nc.vector.tensor_copy(
                dst.rearrange("p (t m) -> p m t", t=PACK), src.rearrange("p (m t) -> p m t", t=PACK)
            )

        def deal_runs(dst, src, run):
            nc.vector.tensor_copy(
                dst.rearrange("p (t a b) -> p a t b", t=PACK, b=run), src.rearrange("p (a t b) -> p a t b", t=PACK, b=run)
            )

        placed1 = zeroed_bytes(H, "placed1")
        placed2 = zeroed_bytes(H, "placed2")

        k1_list = load_list(k1, "k1_list")
        d_bytes = load_scale_rows("d_bytes", d_scales, G)
        offs_list = load_list(offs, "offs_list")
        x_bytes = tile([P, T], U8, "x_bytes")
        for q in range(4):
            rows = x_scales[0].bitcast(I32)[4 * q : 4 * q + 4, :]
            nc.sync.dma_start(
                x_bytes[:].bitcast(I32)[32 * q : 32 * q + 32, :], rows.unsqueeze(0).to_broadcast([8, 4, T // 4])
            )
        d_table = tile([P, G], I32, "d_table")
        nc.sync.dma_start(d_table[:], d_words[0].rearrange("p n t -> p (n t)").bitcast(I32))
        x_table = tile_at(4 * PAGE_BYTES, [P, T], I32, "x_table")
        nc.sync.dma_start(x_table[:], x_words[0].rearrange("p n t -> p (n t)").bitcast(I32))
        k2_list = load_list(k2, "k2_list")
        n1_list = load_list(n1, "n1_list")
        n2_list = load_list(n2, "n2_list")

        warm_in = tile([P, 1], F32, "warm_in")
        nc.vector.memset(warm_in[:], 0.0)
        warm = tile([P, 1], F32, "warm")
        nc.scalar.activation(warm[:], warm_in[:], SIGMOID)

        w1_bytes = tile_at(5 * PAGE_BYTES, [P, H], U8, "w1_bytes")
        nc.vector.tensor_copy(w1_bytes[:], d_bytes[:].indirect(k1_list[:]))
        staged1 = tile_at(PAGE_BYTES - 256, [P, H], U8, "staged1")
        deal(staged1[:], w1_bytes[:])
        move_rows(nc.scalar, placed1, staged1)
        gain = tile_at(5 * PAGE_BYTES, [P, PACK], F32, "gain")
        nc.scalar.dma_start(gain[:], gs.rearrange("(p t) o -> p (t o)", t=PACK))
        xq_bytes = tile([P, S], U8, "xq_bytes")
        nc.vector.tensor_copy(xq_bytes[:], x_bytes[:].indirect(offs_list[:]))
        w1_picked = tile([P, H], U32, "w1_picked")
        nc.vector.tensor_copy(w1_picked[:], d_table[:].bitcast(U32).indirect(k1_list[:]))
        w1_codes = tile([P, H], U32, "w1_codes")
        deal(w1_codes[:], w1_picked[:])
        x_codes = tile([P, S], U32, "x_codes")
        nc.vector.tensor_copy(x_codes[:], x_table[:].bitcast(U32).indirect(offs_list[:]))

        mem_rows = mem.rearrange("(a t b) u -> t a b u", t=PACK, b=RUN)
        out_rows = out.rearrange("(a t b) u -> t a b u", t=PACK, b=RUN)
        pages = []

        def load_page(t):
            page = tile_at(t * PAGE_BYTES, [P, U], F32, "page%d" % t)
            nc.sync.dma_start(page[:], mem_rows[t])
            pages.append(page)

        load_page(0)
        load_page(1)

        h_rows = []
        for t in range(PACK):
            cols = slice(P * t, P * (t + 1))
            acc = psum.tile([P, S], F32, name="h_bank%d" % t)
            nc.tensor.matmul_mx(
                acc[:], lhsT=w1_codes[:, cols].bitcast(FP8X4), lhsT_scale=placed1[:, cols],
                rhs=x_codes[:].bitcast(FP8X4), rhs_scale=xq_bytes[:], start=True, stop=True,
            )
            h_t = tile([P, S], F32, "h_row%d" % t)
            if t == 1:
                nc.vector.tensor_scalar(h_t[:], acc[:], SIXTEENTH, None, MULT)
            else:
                nc.scalar.activation(h_t[:], acc[:], COPY, scale=SIXTEENTH)
            h_rows.append(h_t)

        w2_bytes = tile_at(4 * PAGE_BYTES, [P, H], U8, "w2_bytes")
        nc.vector.tensor_copy(w2_bytes[:], d_bytes[:].indirect(k2_list[:]))
        staged2 = tile_at(3 * PAGE_BYTES - 256, [P, H], U8, "staged2")
        deal_runs(staged2[:].bitcast(I32), w2_bytes[:].bitcast(I32), RUN // 4)
        move_rows(nc.sync, placed2, staged2)
        w2_picked = tile_at(4 * PAGE_BYTES + 512, [P, H], U32, "w2_picked")
        nc.vector.tensor_copy(w2_picked[:], d_table[:].bitcast(U32).indirect(k2_list[:]))
        w2_codes = tile([P, H], U32, "w2_codes")
        deal_runs(w2_codes[:], w2_picked[:], RUN)
        load_page(2)
        load_page(3)

        def weigh(engine, j0, n, weighted):
            for t in range(PACK):
                if engine is nc.vector:
                    nc.vector.tensor_scalar(weighted[:, t, :], h_rows[t][:, j0 : j0 + n], gain[:, t : t + 1], None, MULT)
                else:
                    nc.gpsimd.tensor_scalar(weighted[:, t, :], h_rows[t][:, j0 : j0 + n], gain[:, t : t + 1], 0.0, MULT, ADD)

        def gate(j0, n, gates):
            for t in range(PACK):
                nc.scalar.activation(
                    gates[:, t, :], h_rows[t][:].indirect(n1_list[:, j0 // 16 : (j0 + n) // 16]), SIGMOID
                )

        def gated(engine, weighted, gates, z):
            engine.tensor_tensor(
                z.rearrange("p (c i) t -> p c t i", i=4),
                weighted.rearrange("p t (c i) -> p c t i", i=4),
                gates.rearrange("p t (c i) -> p c t i", i=4),
                MULT,
            )

        def quantise(c, n, z, z_codes):
            z_scales = tile([P, n], U8, "z_scales%d" % c)
            nc.vector.quantize_mx(z_codes[:].bitcast(FP8X4), z_scales[:], z[:].rearrange("p n t -> p (n t)"))
            return z_scales

        def product(acc, t, z_codes, z_scales):
            cols = slice(P * t, P * (t + 1))
            nc.tensor.matmul_mx(
                acc, lhsT=w2_codes[:, cols].bitcast(FP8X4), lhsT_scale=placed2[:, cols],
                rhs=z_codes[:].bitcast(FP8X4), rhs_scale=z_scales[:], start=True, stop=True,
            )

        def scatter(j0, n, t, values):
            nc.vector.tensor_copy(pages[t][:].indirect(n2_list[:, j0 // 16 : (j0 + n) // 16]), values)

        base = 6 * PAGE_BYTES
        weighted0 = tile([P, PACK, 128], F32, "weighted0")
        weigh(nc.vector, 0, 128, weighted0)
        gates0 = tile_at(base, [P, PACK, 128], F32, "gates0")
        gate(0, 128, gates0)
        gates1 = tile_at(4 * PAGE_BYTES + 512, [P, PACK, 128], F32, "gates1")
        gate(128, 128, gates1)
        z0 = tile([P, 128, PACK], BF16, "z0")
        codes0 = tile_at(base + PAGE_BYTES, [P, 128], U32, "codes0")
        gated(nc.vector, weighted0[:], gates0[:], z0[:])
        scales0 = quantise(0, 128, z0, codes0)
        h2_0 = []
        for t in range(PACK):
            acc = psum.tile([P, 128], F32, name="h2_bank0_%d" % t, tag="h_bank%d" % t)
            product(acc[:], t, codes0, scales0)
            values = tile([P, 128], F32, "h2_0_%d" % t)
            nc.scalar.activation(values[:], acc[:], COPY, scale=SIXTEENTH)
            h2_0.append(values)
        weighted1 = tile_at(base, [P, PACK, 128], F32, "weighted1")
        weigh(nc.vector, 128, 128, weighted1)
        z1 = tile_at(base + PAGE_BYTES + 1024, [P, 128, PACK], BF16, "z1")
        codes1 = tile_at(base + 2 * PAGE_BYTES + 2048 - 256, [P, 128], U32, "codes1")
        gated(nc.vector, weighted1[:], gates1[:], z1[:])
        scales1 = quantise(1, 128, z1, codes1)
        acc1a = psum.tile([P, 3, 128], F32, name="h2_bank1a")
        acc1b = psum.tile([P, 128], F32, name="h2_bank1b")
        for t in range(PACK - 1):
            product(acc1a[:, t, :], t, codes1, scales1)
        product(acc1b[:], PACK - 1, codes1, scales1)
        weighted2 = tile_at(base + PAGE_BYTES, [P, PACK, 256], F32, "weighted2")
        weigh(nc.gpsimd, 256, 256, weighted2)
        h2_1a = tile_at(base + 3 * PAGE_BYTES, [P, 3, 128], F32, "h2_1a")
        nc.scalar.activation(h2_1a[:], acc1a[:], COPY, scale=SIXTEENTH)
        gates2 = tile_at(base + 2 * PAGE_BYTES, [P, PACK, 128], F32, "gates2")
        gate(256, 128, gates2)
        gates3 = tile_at(base + 2 * PAGE_BYTES + 2048, [P, PACK, 128], F32, "gates3")
        gate(384, 128, gates3)
        for t in range(PACK):
            scatter(0, 128, t, h2_0[t][:])
        z2 = tile([P, 256, PACK], BF16, "z2")
        gated(nc.gpsimd, weighted2[:, :, :128], gates2[:], z2[:, :128, :])
        gated(nc.gpsimd, weighted2[:, :, 128:], gates3[:], z2[:, 128:, :])
        for t in range(PACK - 1):
            scatter(128, 128, t, h2_1a[:, t, :])
        codes2 = tile_at(base + 3 * PAGE_BYTES, [P, 256], U32, "codes2")
        scales2 = quantise(2, 256, z2, codes2)
        h2_1b = tile_at(base + 2 * PAGE_BYTES + 2048, [P, 128], F32, "h2_1b")
        nc.scalar.activation(h2_1b[:], acc1b[:], COPY, scale=SIXTEENTH)
        h2_2 = []
        for t in range(PACK):
            acc = psum.tile([P, 256], F32, name="h2_bank2_%d" % t, tag="h_bank%d" % t)
            product(acc[:], t, codes2, scales2)
            values = tile([P, 256], F32, "h2_2_%d" % t)
            nc.scalar.activation(values[:], acc[:], COPY, scale=SIXTEENTH)
            h2_2.append(values)
        scatter(128, 128, PACK - 1, h2_1b[:])
        for t in range(PACK):
            scatter(256, 256, t, h2_2[t][:])
            nc.sync.dma_start(out_rows[t], pages[t][:])
